import numpy as np
import ml_dtypes


def mxq(x, axis, fmt="e4m3"):
    dtype, down = {"e4m3": (ml_dtypes.float8_e4m3fn, 7), "e5m2": (ml_dtypes.float8_e5m2, 14)}[fmt]
    v = np.moveaxis(np.asarray(x, np.float32).astype(ml_dtypes.bfloat16).astype(np.float64), axis, -1)
    blocks = v.reshape(v.shape[:-1] + (-1, 32))
    amax = np.abs(blocks).max(-1, keepdims=True)
    byte = np.maximum(np.where(amax > 0, np.frexp(amax)[1] - 1 + 127, 0) - down, 1)
    scale = np.exp2(byte - 127.0)
    codes = (blocks / scale).astype(np.float32).astype(dtype).astype(np.float64)
    return np.moveaxis((codes * scale).reshape(v.shape), -1, axis)


WIDE = False


def mx_kscale(k):
    if not WIDE:
        return np.ones(k)
    levels = np.array([10, -10, 5, -5, 0])
    if k % 512:
        return np.exp2(np.random.permutation(np.resize(levels, k // 32))).repeat(32)
    a = np.empty((k // 512, 16))
    for p in range(k // 512):
        a[p, :8] = np.random.permutation(np.resize(levels, 8))
        for g in range(8):
            far = levels[np.abs(levels - a[p, g]) >= 10]
            a[p, g + 8] = far[np.random.randint(len(far))]
    return np.exp2(a.ravel()).repeat(32)


def f64(x):
    return np.asarray(x).astype(np.float64)


def striped(idx):
    return np.tile(idx.reshape(-1, 16).T, (8, 1)).astype(np.uint16)


def unstriped(offs):
    return offs[:16].T.reshape(-1).astype(np.int64)


def silu(v):
    return v / (1.0 + np.exp(-np.maximum(v, -700.0)))


K, T, E, C, N = 1536, 1024, 24, 128, 128
TOP = 3


def by_expert(wq, xq):
    return np.concatenate([wq[e].T @ xq[:, e * C:(e + 1) * C] for e in range(E)], axis=1)


def setup_inputs():
    n = np.random.standard_normal
    s = mx_kscale(K)[:, None]
    deal = np.repeat(np.arange(E), C).reshape(TOP, T)[:, np.random.permutation(T)]
    deal = np.take_along_axis(deal, np.argsort(np.random.rand(TOP, T), axis=0), axis=0)
    for _ in range(8):
        s_, t_ = np.random.permutation(T).reshape(2, -1); r = np.random.randint(TOP, size=T // 2); x, y = deal[r, s_].copy(), deal[r, t_].copy()
        ok = ~((deal[:, s_] == y).any(0) | (deal[:, t_] == x).any(0)); deal[r[ok], s_[ok]] = y[ok]; deal[r[ok], t_[ok]] = x[ok]
    order = np.lexsort((np.random.rand(TOP * T), deal.reshape(-1)))
    slot_token = order % T; pos = np.empty(TOP * T, np.int64); pos[order] = np.arange(TOP * T); pos = pos.reshape(TOP, T)
    g = np.random.uniform(0.5, 1.5, (TOP, T)); g = g / g.sum(0)
    w_slot = np.empty(E * C)
    for r in range(TOP): w_slot[pos[r]] = g[r]
    return {
        "xT": (n((K, T)) * s).astype(np.float32),
        "w": (n((E, K, N)) / np.sqrt(K) / s[None]).astype(np.float32),
        "b": (0.3 * n((N, E))).astype(np.float32),
        "gate": np.tile(w_slot, (K, 1)).astype(np.float32),
        "offs": striped(slot_token),
        "pos1": striped(pos[0]),
        "pos2": striped(pos[1]),
        "pos3": striped(pos[2]),
    }


def reference(xT, w, b, gate, offs, pos1, pos2, pos3):
    idx = unstriped(offs)
    xq = mxq(f64(gate) * f64(xT)[:, idx], 0, "e4m3")
    y = by_expert(mxq(f64(w), 1, "e4m3"), xq)
    y = silu(y + np.repeat(f64(b), C, axis=1))
    return y[:, unstriped(pos1)] + y[:, unstriped(pos2)] + y[:, unstriped(pos3)]

@@ -1,0 +1,180 @@
+from contextlib import ExitStack
+
+import concourse.mybir as mybir
+
+K, T, E, C, N = 1536, 1024, 24, 128, 128
+S = E * C
+FLOPS = 2 * K * N * S
+BYTES = 4 * (K * T + E * K * N + N * E + S + N * T) + 2 * 128 * (S + 3 * T) // 16
+
+F32 = mybir.dt.float32
+BF16 = mybir.dt.bfloat16
+U32 = mybir.dt.uint32
+U16 = mybir.dt.uint16
+U8 = mybir.dt.uint8
+FP8X4 = mybir.dt.float8_e4m3fn_x4
+MULT = mybir.AluOpType.mult
+ADD = mybir.AluOpType.add
+SILU = mybir.ActivationFunctionType.Silu
+
+P = 128
+PACK = 4
+K_PASS = P * PACK
+PASSES = K // K_PASS
+CHUNK = 512
+EPC = CHUNK // C
+CHUNKS = S // CHUNK
+
+
+def tile_moe_pre_lin_silu_kernel(tc, xT, w, b, gate, offs, pos1, pos2, pos3, out):
+    nc = tc.nc
+    with ExitStack() as ctx:
+        keep = ctx.enter_context(tc.tile_pool(name="keep", bufs=1))
+        xpool = ctx.enter_context(tc.tile_pool(name="xrows", bufs=8))
+        ring = ctx.enter_context(tc.tile_pool(name="ring", bufs=3))
+        psum = ctx.enter_context(tc.psum_pool(name="psum", bufs=8))
+
+        slot_tok = keep.tile([P, S // 16], U16, name="slot_tok")
+        pos = [keep.tile([P, T // 16], U16, name="pos%d" % r) for r in range(3)]
+        gates = [keep.tile([P, CHUNK], F32, name="gate%d" % c) for c in range(CHUNKS)]
+        bias = keep.tile([P, E], F32, name="bias")
+        y = keep.tile([P, S], F32, name="y")
+
+        x_rows = {}
+        w_raw = {}
+        w_bf = {}
+        w_q = {}
+        x_bf = {}
+        x_q = {}
+
+        def load_x(g, j):
+            t = xpool.tile([P, T], F32, name="x_row")
+            src = xT[g * K_PASS:(g + 1) * K_PASS, :].rearrange("(p j) t -> p j t", j=PACK)
+            nc.sync.dma_start(out=t[:], in_=src[:, j, :])
+            x_rows[g, j] = t
+
+        def load_gate(c):
+            nc.sync.dma_start(out=gates[c][:], in_=gate[0:P, c * CHUNK:(c + 1) * CHUNK])
+
+        def load_w(i):
+            g, c = divmod(i, CHUNKS)
+            t = ring.tile([P, EPC, PACK, N], F32, name="w_raw")
+            src = w[c * EPC:(c + 1) * EPC, g * K_PASS:(g + 1) * K_PASS, :].rearrange("e (p j) n -> p e (j n)", j=PACK)
+            nc.sync.dma_start(out=t[:].rearrange("p e j n -> p e (j n)"), in_=src)
+            w_raw[i] = t
+
+        def cast_w(i):
+            t = ring.tile([P, EPC * N * PACK], BF16, name="w_bf", align_bytes=64)
+            nc.scalar.copy(
+                out=t[:].rearrange("p (e c i j) -> p e c j i", e=EPC, i=4, j=PACK),
+                in_=w_raw[i][:].rearrange("p e j (c i) -> p e c j i", i=4),
+            )
+            w_bf[i] = t
+
+        def quant(src, width, name):
+            codes = keep.tile([P, width], U32, name=name + "_codes", align_bytes=64)
+            scales = keep.tile([P, width], U8, name=name + "_scales", align_bytes=64)
+            nc.vector.quantize_mx(out=codes[:].bitcast(FP8X4), scales=scales[:], in_=src[:])
+            return codes, scales
+
+        def quant_w(i):
+            w_q[i] = quant(w_bf[i], EPC * N, "w%d" % i)
+
+        units = []
+        for g in range(PASSES):
+            for c in range(CHUNKS):
+                if g == PASSES - 1 and c == CHUNKS - 1:
+                    units.extend([(g, c * CHUNK, 256), (g, c * CHUNK + 256, 128), (g, c * CHUNK + 384, 128)])
+                else:
+                    units.append((g, c * CHUNK, CHUNK))
+
+        def gather(u):
+            g, s0, n = units[u]
+            c, o = divmod(s0, CHUNK)
+            t = ring.tile([P, PACK, n], F32, name="gathered")
+            for j in range(PACK):
+                nc.vector.tensor_tensor(
+                    t[:, j, :],
+                    x_rows[g, j][:].indirect(slot_tok[:, s0 // 16:(s0 + n) // 16]),
+                    gates[c][:, o:o + n],
+                    MULT,
+                )
+            tb = ring.tile([P, n * PACK], BF16, name="x_bf", align_bytes=64)
+            nc.scalar.copy(
+                out=tb[:].rearrange("p (c i j) -> p c j i", i=4, j=PACK),
+                in_=t[:].rearrange("p j (c i) -> p c j i", i=4),
+            )
+            x_bf[u] = tb
+
+        def quant_x(u):
+            g, s0, n = units[u]
+            codes, scales = quant(x_bf[u], n, "x%d" % u)
+            for e in range(s0 // C, (s0 + n) // C):
+                cols = slice(e * C - s0, (e + 1) * C - s0)
+                x_q[g, e] = (codes[:, cols], scales[:, cols])
+
+        def expert(e):
+            acc = psum.tile([N, C], F32, name="acc")
+            c, el = divmod(e, EPC)
+            cols = slice(el * N, (el + 1) * N)
+            for g in range(PASSES):
+                wc, ws = w_q[g * CHUNKS + c]
+                xc, xs = x_q[g, e]
+                nc.tensor.matmul_mx(
+                    out=acc[:],
+                    lhsT=wc[:, cols].bitcast(FP8X4),
+                    lhsT_scale=ws[:, cols],
+                    rhs=xc.bitcast(FP8X4),
+                    rhs_scale=xs,
+                    start=(g == 0),
+                    stop=(g == PASSES - 1),
+                )
+            nc.scalar.activation(out=y[:, e * C:(e + 1) * C], in_=acc[:], func=SILU, bias=bias[:, e:e + 1])
+
+        def finish(u):
+            quant_x(u)
+            g, s0, n = units[u]
+            if g == PASSES - 1:
+                for e in range(s0 // C, (s0 + n) // C):
+                    expert(e)
+
+        n_w = PASSES * CHUNKS
+        nc.sync.dma_start(slot_tok[:], offs)
+        load_x(0, 0)
+        load_gate(0)
+        for j in range(1, PACK):
+            load_x(0, j)
+        load_w(0)
+        load_gate(1)
+        load_w(1)
+        for u in range(len(units)):
+            if u + 2 < CHUNKS:
+                load_gate(u + 2)
+            if u + 2 < n_w:
+                load_w(u + 2)
+            g_next, c_next = divmod(u, CHUNKS)
+            if g_next + 1 < PASSES and c_next < PACK:
+                load_x(g_next + 1, c_next)
+            if u == 5:
+                nc.sync.dma_start(out=bias[:], in_=b)
+                for r, lst in enumerate((pos1, pos2, pos3)):
+                    nc.sync.dma_start(pos[r][:], lst)
+            if u == 0:
+                cast_w(0)
+            gather(u)
+            if u + 1 < n_w:
+                cast_w(u + 1)
+            if u < n_w:
+                quant_w(u)
+            if u > 0:
+                finish(u - 1)
+        finish(len(units) - 1)
+
+        first = ring.tile([P, T], F32, name="gathered")
+        second = ring.tile([P, T], F32, name="gathered")
+        nc.vector.tensor_copy(first[:], y[:].indirect(pos[0][:]))
+        nc.vector.tensor_tensor(second[:], y[:].indirect(pos[1][:]), first[:], ADD)
+        for t0, n in ((0, 512), (512, 384), (896, 128)):
+            res = keep.tile([P, n], F32, name="res%d" % t0)
+            nc.vector.tensor_tensor(res[:], y[:].indirect(pos[2][:, t0 // 16:(t0 + n) // 16]), second[:, t0:t0 + n], ADD)
+            nc.sync.dma_start(out=out[:, t0:t0 + n], in_=res[:])

@@ -21,104 +21,118 @@ P = 128
 PACK = 4
 K_PASS = P * PACK
 PASSES = K // K_PASS
-CHUNK = 512
-EPC = CHUNK // C
-CHUNKS = S // CHUNK
+WINDOW = 1552
+W_LOAD = 4
+W_GROUP = 8
+W_AHEAD = 3
+UNITS = (
+    (0, 0, 512), (0, 512, 1024), (0, 1536, 1536), (1, 0, 1536), (1, 1536, 1536), (2, 0, 1536), (2, 1536, 768), (2, 2304, 512), (2, 2816, 256),
+)
+W_PER_UNIT = (1, 1, 2, 2, 2, 1, 0, 0, 0)
+GATE_PIECES = ((0, 512), (512, 1024), (1536, 1536))
+
+
+def pieces(s0, n):
+    res = []
+    while n > 0:
+        m = 1024
+        while m > n:
+            m = m // 2
+        res.append((s0, m))
+        s0 = s0 + m
+        n = n - m
+    return res
 
 
 def tile_moe_pre_lin_silu_kernel(tc, xT, w, b, gate, offs, pos1, pos2, pos3, out):
     nc = tc.nc
     with ExitStack() as ctx:
         keep = ctx.enter_context(tc.tile_pool(name="keep", bufs=1))
-        xpool = ctx.enter_context(tc.tile_pool(name="xrows", bufs=8))
-        ring = ctx.enter_context(tc.tile_pool(name="ring", bufs=3))
+        ring = ctx.enter_context(tc.tile_pool(name="ring", bufs=2))
+        wring = ctx.enter_context(tc.tile_pool(name="wring", bufs=W_AHEAD))
         psum = ctx.enter_context(tc.psum_pool(name="psum", bufs=8))
 
         slot_tok = keep.tile([P, S // 16], U16, name="slot_tok")
         pos = [keep.tile([P, T // 16], U16, name="pos%d" % r) for r in range(3)]
-        gates = [keep.tile([P, CHUNK], F32, name="gate%d" % c) for c in range(CHUNKS)]
+        gates = keep.tile([P, S], F32, name="gates")
+        windows = [keep.tile([P, WINDOW], F32, name="window%d" % j) for j in range(PACK)]
         bias = keep.tile([P, E], F32, name="bias")
         y = keep.tile([P, S], F32, name="y")
 
-        x_rows = {}
+        parts = W_GROUP // W_LOAD
+        n_loads = PASSES * E // W_LOAD
         w_raw = {}
-        w_bf = {}
         w_q = {}
         x_bf = {}
         x_q = {}
+        ready = []
 
         def load_x(g, j):
-            t = xpool.tile([P, T], F32, name="x_row")
             src = xT[g * K_PASS:(g + 1) * K_PASS, :].rearrange("(p j) t -> p j t", j=PACK)
-            nc.sync.dma_start(out=t[:], in_=src[:, j, :])
-            x_rows[g, j] = t
+            nc.sync.dma_start(out=windows[j][:, 0:T], in_=src[:, j, :])
 
-        def load_gate(c):
-            nc.sync.dma_start(out=gates[c][:], in_=gate[0:P, c * CHUNK:(c + 1) * CHUNK])
+        def load_gate(i):
+            s0, n = GATE_PIECES[i]
+            nc.sync.dma_start(out=gates[:, s0:s0 + n], in_=gate[0:P, s0:s0 + n])
 
-        def load_w(i):
-            g, c = divmod(i, CHUNKS)
-            t = ring.tile([P, EPC, PACK, N], F32, name="w_raw")
-            src = w[c * EPC:(c + 1) * EPC, g * K_PASS:(g + 1) * K_PASS, :].rearrange("e (p j) n -> p e (j n)", j=PACK)
-            nc.sync.dma_start(out=t[:].rearrange("p e j n -> p e (j n)"), in_=src)
-            w_raw[i] = t
+        def load_w(q, queue):
+            i, part = divmod(q, parts)
+            eg, g = divmod(i, PASSES)
+            e0 = eg * W_GROUP + part * W_LOAD
+            raw = wring.tile([P, W_LOAD, PACK, N], F32, name="w_raw")
+            src = w[e0:e0 + W_LOAD, g * K_PASS:(g + 1) * K_PASS, :].rearrange("e (p j) n -> p e (j n)", j=PACK)
+            queue.dma_start(out=raw[:].rearrange("p e j n -> p e (j n)"), in_=src)
+            w_raw[q] = raw
 
-        def cast_w(i):
-            t = ring.tile([P, EPC * N * PACK], BF16, name="w_bf", align_bytes=64)
-            nc.scalar.copy(
-                out=t[:].rearrange("p (e c i j) -> p e c j i", e=EPC, i=4, j=PACK),
-                in_=w_raw[i][:].rearrange("p e j (c i) -> p e c j i", i=4),
-            )
-            w_bf[i] = t
-
-        def quant(src, width, name):
-            codes = keep.tile([P, width], U32, name=name + "_codes", align_bytes=64)
-            scales = keep.tile([P, width], U8, name=name + "_scales", align_bytes=64)
+        def quant(pool, src, width, name):
+            codes = pool.tile([P, width], U32, name=name + "_codes", align_bytes=64)
+            scales = pool.tile([P, width], U8, name=name + "_scales", align_bytes=64)
             nc.vector.quantize_mx(out=codes[:].bitcast(FP8X4), scales=scales[:], in_=src[:])
             return codes, scales
 
-        def quant_w(i):
-            w_q[i] = quant(w_bf[i], EPC * N, "w%d" % i)
-
-        units = []
-        for g in range(PASSES):
-            for c in range(CHUNKS):
-                if g == PASSES - 1 and c == CHUNKS - 1:
-                    units.extend([(g, c * CHUNK, 256), (g, c * CHUNK + 256, 128), (g, c * CHUNK + 384, 128)])
-                else:
-                    units.append((g, c * CHUNK, CHUNK))
+        def weights(i):
+            t = ring.tile([P, W_GROUP * N * PACK], BF16, name="w_bf", align_bytes=64)
+            width = W_LOAD * N * PACK
+            for part in range(parts):
+                q = i * parts + part
+                nc.scalar.copy(
+                    out=t[:, part * width:(part + 1) * width].rearrange("p (e c i j) -> p e c j i", e=W_LOAD, i=4, j=PACK),
+                    in_=w_raw[q][:].rearrange("p e j (c i) -> p e c j i", i=4),
+                )
+                if q + W_AHEAD < n_loads:
+                    load_w(q + W_AHEAD, nc.scalar)
+            w_q[i] = quant(keep, t, W_GROUP * N, "w%d" % i)
 
         def gather(u):
-            g, s0, n = units[u]
-            c, o = divmod(s0, CHUNK)
+            g, s0, n = UNITS[u]
             t = ring.tile([P, PACK, n], F32, name="gathered")
             for j in range(PACK):
                 nc.vector.tensor_tensor(
                     t[:, j, :],
-                    x_rows[g, j][:].indirect(slot_tok[:, s0 // 16:(s0 + n) // 16]),
-                    gates[c][:, o:o + n],
+                    windows[j][:].indirect(slot_tok[:, s0 // 16:(s0 + n) // 16]),
+                    gates[:, s0:s0 + n],
                     MULT,
                 )
-            tb = ring.tile([P, n * PACK], BF16, name="x_bf", align_bytes=64)
-            nc.scalar.copy(
-                out=tb[:].rearrange("p (c i j) -> p c j i", i=4, j=PACK),
-                in_=t[:].rearrange("p j (c i) -> p c j i", i=4),
-            )
-            x_bf[u] = tb
+                if s0 + n == S and g + 1 < PASSES:
+                    load_x(g + 1, j)
+            return t
 
-        def quant_x(u):
-            g, s0, n = units[u]
-            codes, scales = quant(x_bf[u], n, "x%d" % u)
-            for e in range(s0 // C, (s0 + n) // C):
-                cols = slice(e * C - s0, (e + 1) * C - s0)
-                x_q[g, e] = (codes[:, cols], scales[:, cols])
+        def cast_x(u, t):
+            g, s0, n = UNITS[u]
+            for p0, m in pieces(s0, n):
+                tb = ring.tile([P, m * PACK], BF16, name="x_bf", align_bytes=64)
+                nc.scalar.copy(
+                    out=tb[:].rearrange("p (c i j) -> p c j i", i=4, j=PACK),
+                    in_=t[:, :, p0 - s0:p0 - s0 + m].rearrange("p j (c i) -> p c j i", i=4),
+                )
+                x_bf[g, p0] = tb
 
         def expert(e):
             acc = psum.tile([N, C], F32, name="acc")
-            c, el = divmod(e, EPC)
+            eg, el = divmod(e, W_GROUP)
             cols = slice(el * N, (el + 1) * N)
             for g in range(PASSES):
-                wc, ws = w_q[g * CHUNKS + c]
+                wc, ws = w_q[eg * PASSES + g]
                 xc, xs = x_q[g, e]
                 nc.tensor.matmul_mx(
                     out=acc[:],
@@ -132,49 +146,58 @@ def tile_moe_pre_lin_silu_kernel(tc, xT, w, b, gate, offs, pos1, pos2, pos3, out
             nc.scalar.activation(out=y[:, e * C:(e + 1) * C], in_=acc[:], func=SILU, bias=bias[:, e:e + 1])
 
         def finish(u):
-            quant_x(u)
-            g, s0, n = units[u]
-            if g == PASSES - 1:
-                for e in range(s0 // C, (s0 + n) // C):
-                    expert(e)
+            g, s0, n = UNITS[u]
+            last = g == PASSES - 1
+            for p0, m in pieces(s0, n):
+                if last:
+                    codes, scales = quant(ring, x_bf[g, p0], m, "x_last")
+                else:
+                    codes, scales = quant(keep, x_bf[g, p0], m, "x%d_%d" % (g, p0))
+                for e in range(p0 // C, (p0 + m) // C):
+                    cols = slice(e * C - p0, (e + 1) * C - p0)
+                    x_q[g, e] = (codes[:, cols], scales[:, cols])
+                    if last:
+                        ready.append(e)
 
-        n_w = PASSES * CHUNKS
+        for j in range(PACK):
+            nc.gpsimd.memset(windows[j][:, T:WINDOW], 0.0)
         nc.sync.dma_start(slot_tok[:], offs)
         load_x(0, 0)
         load_gate(0)
         for j in range(1, PACK):
             load_x(0, j)
-        load_w(0)
         load_gate(1)
-        load_w(1)
-        for u in range(len(units)):
-            if u + 2 < CHUNKS:
-                load_gate(u + 2)
-            if u + 2 < n_w:
-                load_w(u + 2)
-            g_next, c_next = divmod(u, CHUNKS)
-            if g_next + 1 < PASSES and c_next < PACK:
-                load_x(g_next + 1, c_next)
-            if u == 5:
-                nc.sync.dma_start(out=bias[:], in_=b)
-                for r, lst in enumerate((pos1, pos2, pos3)):
-                    nc.sync.dma_start(pos[r][:], lst)
-            if u == 0:
-                cast_w(0)
-            gather(u)
-            if u + 1 < n_w:
-                cast_w(u + 1)
-            if u < n_w:
-                quant_w(u)
+        load_w(0, nc.sync)
+        load_w(1, nc.sync)
+        load_gate(2)
+        for q in range(2, W_AHEAD):
+            load_w(q, nc.sync)
+        nc.sync.dma_start(out=bias[:], in_=b)
+        for r, lst in enumerate((pos1, pos2, pos3)):
+            nc.sync.dma_start(pos[r][:], lst)
+
+        w_done = 0
+        for u in range(len(UNITS)):
+            t = gather(u)
+            if u == 4:
+                warm = keep.tile([P, 1], F32, name="warm")
+                nc.scalar.activation(out=warm[:], in_=bias[:, 0:1], func=SILU)
+            for i in range(w_done, w_done + W_PER_UNIT[u]):
+                weights(i)
+            w_done = w_done + W_PER_UNIT[u]
             if u > 0:
                 finish(u - 1)
-        finish(len(units) - 1)
+            cast_x(u, t)
+            for e in ready:
+                expert(e)
+            ready.clear()
+        finish(len(UNITS) - 1)
+        for e in ready:
+            expert(e)
 
-        first = ring.tile([P, T], F32, name="gathered")
-        second = ring.tile([P, T], F32, name="gathered")
-        nc.vector.tensor_copy(first[:], y[:].indirect(pos[0][:]))
-        nc.vector.tensor_tensor(second[:], y[:].indirect(pos[1][:]), first[:], ADD)
-        for t0, n in ((0, 512), (512, 384), (896, 128)):
-            res = keep.tile([P, n], F32, name="res%d" % t0)
-            nc.vector.tensor_tensor(res[:], y[:].indirect(pos[2][:, t0 // 16:(t0 + n) // 16]), second[:, t0:t0 + n], ADD)
-            nc.sync.dma_start(out=out[:, t0:t0 + n], in_=res[:])
+        sums = ring.tile([P, 3, T], F32, name="gathered")
+        nc.vector.tensor_copy(sums[:, 0, :], y[:].indirect(pos[0][:]))
+        nc.vector.tensor_tensor(sums[:, 1, :], y[:].indirect(pos[1][:]), sums[:, 0, :], ADD)
+        for t0, n in ((0, 768), (768, 256)):
+            nc.vector.tensor_tensor(sums[:, 2, t0:t0 + n], y[:].indirect(pos[2][:, t0 // 16:(t0 + n) // 16]), sums[:, 1, t0:t0 + n], ADD)
+            nc.sync.dma_start(out=out[:, t0:t0 + n], in_=sums[:, 2, t0:t0 + n])

@@ -26,9 +26,9 @@ W_LOAD = 4
 W_GROUP = 8
 W_AHEAD = 3
 UNITS = (
-    (0, 0, 512), (0, 512, 1024), (0, 1536, 1536), (1, 0, 1536), (1, 1536, 1536), (2, 0, 1536), (2, 1536, 768), (2, 2304, 512), (2, 2816, 256),
+    (0, 0, 512), (0, 512, 1024), (0, 1536, 1536), (1, 0, 1536), (1, 1536, 1536), (2, 0, 1536), (2, 1536, 768), (2, 2304, 384), (2, 2688, 256), (2, 2944, 128),
 )
-W_PER_UNIT = (1, 1, 2, 2, 2, 1, 0, 0, 0)
+W_PER_UNIT = (1, 1, 2, 2, 2, 1, 0, 0, 0, 0)
 GATE_PIECES = ((0, 512), (512, 1024), (1536, 1536))
 
 
@@ -58,6 +58,7 @@ def tile_moe_pre_lin_silu_kernel(tc, xT, w, b, gate, offs, pos1, pos2, pos3, out
         windows = [keep.tile([P, WINDOW], F32, name="window%d" % j) for j in range(PACK)]
         bias = keep.tile([P, E], F32, name="bias")
         y = keep.tile([P, S], F32, name="y")
+        planes = keep.tile([P, 2 * PACK - 1, 1536], F32, name="planes")
 
         parts = W_GROUP // W_LOAD
         n_loads = PASSES * E // W_LOAD
@@ -105,10 +106,11 @@ def tile_moe_pre_lin_silu_kernel(tc, xT, w, b, gate, offs, pos1, pos2, pos3, out
 
         def gather(u):
             g, s0, n = UNITS[u]
-            t = ring.tile([P, PACK, n], F32, name="gathered")
-            for j in range(PACK):
+            first = (u % 2) * (PACK - 1)
+            t = planes[:, first:first + PACK, 0:n]
+            for j in (range(PACK) if u % 2 == 0 else (1, 2, 3, 0)):
                 nc.vector.tensor_tensor(
-                    t[:, j, :],
+                    planes[:, first + j, 0:n],
                     windows[j][:].indirect(slot_tok[:, s0 // 16:(s0 + n) // 16]),
                     gates[:, s0:s0 + n],
                     MULT,
@@ -195,9 +197,11 @@ def tile_moe_pre_lin_silu_kernel(tc, xT, w, b, gate, offs, pos1, pos2, pos3, out
         for e in ready:
             expert(e)
 
-        sums = ring.tile([P, 3, T], F32, name="gathered")
-        nc.vector.tensor_copy(sums[:, 0, :], y[:].indirect(pos[0][:]))
-        nc.vector.tensor_tensor(sums[:, 1, :], y[:].indirect(pos[1][:]), sums[:, 0, :], ADD)
-        for t0, n in ((0, 768), (768, 256)):
-            nc.vector.tensor_tensor(sums[:, 2, t0:t0 + n], y[:].indirect(pos[2][:, t0 // 16:(t0 + n) // 16]), sums[:, 1, t0:t0 + n], ADD)
-            nc.sync.dma_start(out=out[:, t0:t0 + n], in_=sums[:, 2, t0:t0 + n])
+        half = T // 2
+        for t0 in (0, half):
+            nc.vector.tensor_copy(planes[:, 0, t0:t0 + half], y[:].indirect(pos[0][:, t0 // 16:(t0 + half) // 16]))
+        for t0 in (0, half):
+            nc.vector.tensor_tensor(planes[:, 1, t0:t0 + half], y[:].indirect(pos[1][:, t0 // 16:(t0 + half) // 16]), planes[:, 0, t0:t0 + half], ADD)
+        for t0, n in ((0, 512), (512, 384), (896, 128)):
+            nc.vector.tensor_tensor(planes[:, 2, t0:t0 + n], y[:].indirect(pos[2][:, t0 // 16:(t0 + n) // 16]), planes[:, 1, t0:t0 + n], ADD)
+            nc.sync.dma_start(out=out[:, t0:t0 + n], in_=planes[:, 2, t0:t0 + n])

from contextlib import ExitStack

import concourse.mybir as mybir

K, T, E, C, N = 1536, 1024, 24, 128, 128
S = E * C
FLOPS = 2 * K * N * S
BYTES = 4 * (K * T + E * K * N + N * E + S + N * T) + 2 * 128 * (S + 3 * T) // 16

F32 = mybir.dt.float32
BF16 = mybir.dt.bfloat16
U32 = mybir.dt.uint32
U16 = mybir.dt.uint16
U8 = mybir.dt.uint8
FP8X4 = mybir.dt.float8_e4m3fn_x4
MULT = mybir.AluOpType.mult
ADD = mybir.AluOpType.add
SILU = mybir.ActivationFunctionType.Silu

P = 128
PACK = 4
K_PASS = P * PACK
PASSES = K // K_PASS
WINDOW = 1552
W_LOAD = 4
W_GROUP = 8
W_AHEAD = 3
UNITS = (
    (0, 0, 512), (0, 512, 1024), (0, 1536, 1536), (1, 0, 1536), (1, 1536, 1536), (2, 0, 1536), (2, 1536, 768), (2, 2304, 384), (2, 2688, 256), (2, 2944, 128),
)
W_PER_UNIT = (1, 1, 2, 2, 2, 1, 0, 0, 0, 0)
GATE_PIECES = ((0, 512), (512, 1024), (1536, 1536))


def pieces(s0, n):
    res = []
    while n > 0:
        m = 1024
        while m > n:
            m = m // 2
        res.append((s0, m))
        s0 = s0 + m
        n = n - m
    return res


def tile_moe_pre_lin_silu_kernel(tc, xT, w, b, gate, offs, pos1, pos2, pos3, out):
    nc = tc.nc
    with ExitStack() as ctx:
        keep = ctx.enter_context(tc.tile_pool(name="keep", bufs=1))
        ring = ctx.enter_context(tc.tile_pool(name="ring", bufs=2))
        wring = ctx.enter_context(tc.tile_pool(name="wring", bufs=W_AHEAD))
        psum = ctx.enter_context(tc.psum_pool(name="psum", bufs=8))

        slot_tok = keep.tile([P, S // 16], U16, name="slot_tok")
        pos = [keep.tile([P, T // 16], U16, name="pos%d" % r) for r in range(3)]
        gates = keep.tile([P, S], F32, name="gates")
        windows = [keep.tile([P, WINDOW], F32, name="window%d" % j) for j in range(PACK)]
        bias = keep.tile([P, E], F32, name="bias")
        y = keep.tile([P, S], F32, name="y")
        planes = keep.tile([P, 2 * PACK - 1, 1536], F32, name="planes")

        parts = W_GROUP // W_LOAD
        n_loads = PASSES * E // W_LOAD
        w_raw = {}
        w_q = {}
        x_bf = {}
        x_q = {}
        ready = []

        def load_x(g, j):
            src = xT[g * K_PASS:(g + 1) * K_PASS, :].rearrange("(p j) t -> p j t", j=PACK)
            nc.sync.dma_start(out=windows[j][:, 0:T], in_=src[:, j, :])

        def load_gate(i):
            s0, n = GATE_PIECES[i]
            nc.sync.dma_start(out=gates[:, s0:s0 + n], in_=gate[0:P, s0:s0 + n])

        def load_w(q, queue):
            i, part = divmod(q, parts)
            eg, g = divmod(i, PASSES)
            e0 = eg * W_GROUP + part * W_LOAD
            raw = wring.tile([P, W_LOAD, PACK, N], F32, name="w_raw")
            src = w[e0:e0 + W_LOAD, g * K_PASS:(g + 1) * K_PASS, :].rearrange("e (p j) n -> p e (j n)", j=PACK)
            queue.dma_start(out=raw[:].rearrange("p e j n -> p e (j n)"), in_=src)
            w_raw[q] = raw

        def quant(pool, src, width, name):
            codes = pool.tile([P, width], U32, name=name + "_codes", align_bytes=64)
            scales = pool.tile([P, width], U8, name=name + "_scales", align_bytes=64)
            nc.vector.quantize_mx(out=codes[:].bitcast(FP8X4), scales=scales[:], in_=src[:])
            return codes, scales

        def weights(i):
            t = ring.tile([P, W_GROUP * N * PACK], BF16, name="w_bf", align_bytes=64)
            width = W_LOAD * N * PACK
            for part in range(parts):
                q = i * parts + part
                nc.scalar.copy(
                    out=t[:, part * width:(part + 1) * width].rearrange("p (e c i j) -> p e c j i", e=W_LOAD, i=4, j=PACK),
                    in_=w_raw[q][:].rearrange("p e j (c i) -> p e c j i", i=4),
                )
                if q + W_AHEAD < n_loads:
                    load_w(q + W_AHEAD, nc.scalar)
            w_q[i] = quant(keep, t, W_GROUP * N, "w%d" % i)

        def gather(u):
            g, s0, n = UNITS[u]
            first = (u % 2) * (PACK - 1)
            t = planes[:, first:first + PACK, 0:n]
            for j in (range(PACK) if u % 2 == 0 else (1, 2, 3, 0)):
                nc.vector.tensor_tensor(
                    planes[:, first + j, 0:n],
                    windows[j][:].indirect(slot_tok[:, s0 // 16:(s0 + n) // 16]),
                    gates[:, s0:s0 + n],
                    MULT,
                )
                if s0 + n == S and g + 1 < PASSES:
                    load_x(g + 1, j)
            return t

        def cast_x(u, t):
            g, s0, n = UNITS[u]
            for p0, m in pieces(s0, n):
                tb = ring.tile([P, m * PACK], BF16, name="x_bf", align_bytes=64)
                nc.scalar.copy(
                    out=tb[:].rearrange("p (c i j) -> p c j i", i=4, j=PACK),
                    in_=t[:, :, p0 - s0:p0 - s0 + m].rearrange("p j (c i) -> p c j i", i=4),
                )
                x_bf[g, p0] = tb

        def expert(e):
            acc = psum.tile([N, C], F32, name="acc")
            eg, el = divmod(e, W_GROUP)
            cols = slice(el * N, (el + 1) * N)
            for g in range(PASSES):
                wc, ws = w_q[eg * PASSES + g]
                xc, xs = x_q[g, e]
                nc.tensor.matmul_mx(
                    out=acc[:],
                    lhsT=wc[:, cols].bitcast(FP8X4),
                    lhsT_scale=ws[:, cols],
                    rhs=xc.bitcast(FP8X4),
                    rhs_scale=xs,
                    start=(g == 0),
                    stop=(g == PASSES - 1),
                )
            nc.scalar.activation(out=y[:, e * C:(e + 1) * C], in_=acc[:], func=SILU, bias=bias[:, e:e + 1])

        def finish(u):
            g, s0, n = UNITS[u]
            last = g == PASSES - 1
            for p0, m in pieces(s0, n):
                if last:
                    codes, scales = quant(ring, x_bf[g, p0], m, "x_last")
                else:
                    codes, scales = quant(keep, x_bf[g, p0], m, "x%d_%d" % (g, p0))
                for e in range(p0 // C, (p0 + m) // C):
                    cols = slice(e * C - p0, (e + 1) * C - p0)
                    x_q[g, e] = (codes[:, cols], scales[:, cols])
                    if last:
                        ready.append(e)

        for j in range(PACK):
            nc.gpsimd.memset(windows[j][:, T:WINDOW], 0.0)
        nc.sync.dma_start(slot_tok[:], offs)
        load_x(0, 0)
        load_gate(0)
        for j in range(1, PACK):
            load_x(0, j)
        load_gate(1)
        load_w(0, nc.sync)
        load_w(1, nc.sync)
        load_gate(2)
        for q in range(2, W_AHEAD):
            load_w(q, nc.sync)
        nc.sync.dma_start(out=bias[:], in_=b)
        for r, lst in enumerate((pos1, pos2, pos3)):
            nc.sync.dma_start(pos[r][:], lst)

        w_done = 0
        for u in range(len(UNITS)):
            t = gather(u)
            if u == 4:
                warm = keep.tile([P, 1], F32, name="warm")
                nc.scalar.activation(out=warm[:], in_=bias[:, 0:1], func=SILU)
            for i in range(w_done, w_done + W_PER_UNIT[u]):
                weights(i)
            w_done = w_done + W_PER_UNIT[u]
            if u > 0:
                finish(u - 1)
            cast_x(u, t)
            for e in ready:
                expert(e)
            ready.clear()
        finish(len(UNITS) - 1)
        for e in ready:
            expert(e)

        half = T // 2
        for t0 in (0, half):
            nc.vector.tensor_copy(planes[:, 0, t0:t0 + half], y[:].indirect(pos[0][:, t0 // 16:(t0 + half) // 16]))
        for t0 in (0, half):
            nc.vector.tensor_tensor(planes[:, 1, t0:t0 + half], y[:].indirect(pos[1][:, t0 // 16:(t0 + half) // 16]), planes[:, 0, t0:t0 + half], ADD)
        for t0, n in ((0, 512), (512, 384), (896, 128)):
            nc.vector.tensor_tensor(planes[:, 2, t0:t0 + n], y[:].indirect(pos[2][:, t0 // 16:(t0 + n) // 16]), planes[:, 1, t0:t0 + n], ADD)
            nc.sync.dma_start(out=out[:, t0:t0 + n], in_=planes[:, 2, t0:t0 + n])
